import numpy as np
import ml_dtypes


def mxq(x, axis, fmt="e4m3"):
    dtype, down = {"e4m3": (ml_dtypes.float8_e4m3fn, 7), "e5m2": (ml_dtypes.float8_e5m2, 14)}[fmt]
    v = np.moveaxis(np.asarray(x, np.float32).astype(ml_dtypes.bfloat16).astype(np.float64), axis, -1)
    blocks = v.reshape(v.shape[:-1] + (-1, 32))
    amax = np.abs(blocks).max(-1, keepdims=True)
    byte = np.maximum(np.where(amax > 0, np.frexp(amax)[1] - 1 + 127, 0) - down, 1)
    scale = np.exp2(byte - 127.0)
    codes = (blocks / scale).astype(np.float32).astype(dtype).astype(np.float64)
    return np.moveaxis((codes * scale).reshape(v.shape), -1, axis)


WIDE = False


def mx_kscale(k):
    if not WIDE:
        return np.ones(k)
    levels = np.array([10, -10, 5, -5, 0])
    if k % 512:
        return np.exp2(np.random.permutation(np.resize(levels, k // 32))).repeat(32)
    a = np.empty((k // 512, 16))
    for p in range(k // 512):
        a[p, :8] = np.random.permutation(np.resize(levels, 8))
        for g in range(8):
            far = levels[np.abs(levels - a[p, g]) >= 10]
            a[p, g + 8] = far[np.random.randint(len(far))]
    return np.exp2(a.ravel()).repeat(32)


def f64(x):
    return np.asarray(x).astype(np.float64)


def striped(idx):
    return np.tile(idx.reshape(-1, 16).T, (8, 1)).astype(np.uint16)


def unstriped(offs):
    return offs[:16].T.reshape(-1).astype(np.int64)


def striped8(idx):
    return np.concatenate([x.reshape(-1, 16).T for x in idx]).astype(np.uint16)


def runs(offs, k):
    lists = np.stack([offs[16 * r : 16 * r + 16].T.reshape(-1) for r in range(8)]).astype(np.int64)
    return lists[np.arange(k) % 512 // 64]


def pack_weight(w):
    k, n = w.shape
    w = f64(np.asarray(w, np.float32).astype(ml_dtypes.bfloat16)).reshape(k // 32, 32, n)
    amax = np.abs(w).max(1)
    byte = np.clip(np.where(amax > 0, np.frexp(amax)[1] - 1 + 127 - 7, 1), 1, 254)
    scaled = (w * np.exp2(127.0 - byte)[:, None, :]).reshape(k, n).astype(np.float32)
    words = np.ascontiguousarray(scaled.reshape(k // 512, 128, 4, n).transpose(0, 1, 3, 2)).astype(ml_dtypes.float8_e4m3fn).view(np.uint8)
    return words, np.ascontiguousarray(byte.astype(np.uint8).reshape(k // 512, 16, n))


def unpack_weight(words, scales):
    g, p, n, _ = words.shape
    vals = np.ascontiguousarray(words).view(ml_dtypes.float8_e4m3fn).astype(np.float64) * np.repeat(np.exp2(scales.astype(np.float64) - 127.0), 8, axis=1)[..., None]
    return vals.transpose(0, 1, 3, 2).reshape(g * 512, n)


K, T, S, H, W, C = 512, 2048, 256, 512, 128, 512


def setup_inputs():
    n = np.random.standard_normal
    s = mx_kscale(K)[:, None]
    packed_xT = pack_weight(n((K, T)) * s)
    perm = np.random.permutation(S)
    return {
        "x_words": packed_xT[0],
        "x_scales": packed_xT[1],
        "w1": (n((K, H)) / np.sqrt(K) / s).astype(np.float32),
        "gs": (np.random.uniform(0.5, 1.5, (K, 1)) / s).astype(np.float32),
        "offs": striped(np.random.permutation(T)[:S]),
        "n1": striped(perm[:W]),
        "n2": striped(perm[W:]),
        "ca": striped(np.random.permutation(T)[:C]),
        "hc": striped8(np.random.randint(0, T, (8, C))),
        "n3": striped8(np.stack([np.random.permutation(S) for _ in range(8)])),
        "n4": striped8(np.stack([np.random.permutation(S) for _ in range(8)])),
    }


def reference(x_words, x_scales, w1, gs, offs, n1, n2, ca, hc, n3, n4):
    x_ca = unpack_weight(x_words, x_scales)[:, unstriped(ca)]
    xq = unpack_weight(x_words, x_scales)[:, unstriped(offs)]
    y = mxq(f64(w1), 0, "e4m3").T @ xq
    pb = y[:, unstriped(n2)]
    pa = y[:, unstriped(n1)]
    rb = pb - (0.5 * pa)
    ra = np.sqrt((pa) ** 2 + (pb) ** 2 + 0.25)
    ds = np.zeros((H, S))
    ds[:, unstriped(n1)] = ra
    dt = ds.copy()
    dt[:, unstriped(n2)] = rb
    z = f64(gs) * dt
    zq = mxq(z, 0, "e4m3")
    a = 0.0625 * (x_ca.T @ zq)
    x_hc = unpack_weight(x_words, x_scales)[np.arange(K)[:, None], runs(hc, K)]
    b = 0.0625 * (x_hc.T @ zq)
    return a[np.arange(C)[:, None], runs(n3, C)] - (np.tanh(b) * (b[np.arange(C)[:, None], runs(n4, C)]))

@@ -1,0 +1,187 @@
+from contextlib import ExitStack
+
+import concourse.mybir as mybir
+
+K, T, S, H, W, C = 512, 2048, 256, 512, 128, 512
+FLOPS = 2 * K * H * S + 2 * 2 * K * C * S
+
+F32 = mybir.dt.float32
+BF16 = mybir.dt.bfloat16
+I32 = mybir.dt.int32
+U32 = mybir.dt.uint32
+U16 = mybir.dt.uint16
+U8 = mybir.dt.uint8
+FP8X4 = mybir.dt.float8_e4m3fn_x4
+ALU = mybir.AluOpType
+ACT = mybir.ActivationFunctionType
+
+P = 128
+PACK = 4
+
+
+def tile_picked_cdhsoftbpolar_none_p_kernel(tc, x_words, x_scales, w1, gs, offs, n1, n2, ca, hc, n3, n4, out):
+    nc = tc.nc
+    with ExitStack() as ctx:
+        keep = ctx.enter_context(tc.tile_pool(name="keep", bufs=1))
+        psum = ctx.enter_context(tc.psum_pool(name="psum", bufs=1))
+
+        def new(shape, dtype, name, tag=None):
+            return keep.tile(shape, dtype, name=name, tag=tag or name, align_bytes=64)
+
+        def load_list(src, name):
+            held = new(list(src.shape), U16, name)
+            nc.sync.dma_start(held[:], src)
+            return held
+
+        def bank(b):
+            return psum.tile([P, S], F32, name="bank%d" % b)
+
+        scale_table = new([P, T], U8, "scale_table")
+        nc.vector.memset(scale_table[:].bitcast(I32), 0)
+        rows = x_scales[0].bitcast(I32)
+        for r, step in ((0, 2), (1, 2), (2, 4), (3, 4)):
+            nc.scalar.dma_start(scale_table[r:P:8 * step, :].bitcast(I32), rows[r:16:step, :])
+        offs_sb = load_list(offs, "offs_sb")
+        hc_sb = load_list(hc, "hc_sb")
+        ca_sb = load_list(ca, "ca_sb")
+        w_raw = new([P, PACK, H], F32, "w_raw")
+        nc.sync.dma_start(w_raw[:], w1.rearrange("(p j) c -> p j c", j=PACK))
+        word_table = new([P, T], I32, "word_table")
+        nc.sync.dma_start(word_table[:], x_words[0].rearrange("p c r -> p (c r)").bitcast(I32))
+        n1_sb = load_list(n1, "n1_sb")
+        n2_sb = load_list(n2, "n2_sb")
+        gs_sb = new([P, PACK], F32, "gs_sb")
+        nc.sync.dma_start(gs_sb[:], gs.rearrange("(p j) o -> p (j o)", j=PACK))
+        n3_sb = load_list(n3, "n3_sb")
+        n4_sb = load_list(n4, "n4_sb")
+
+        def gather_scales(lst, n, name, tag=None):
+            got = new([P, n], U8, name, tag)
+            nc.vector.tensor_copy(got[:], scale_table[:].indirect(lst[:]))
+            return got
+
+        def gather_words(lst, n, name, tag=None):
+            got = new([P, n], U32, name, tag)
+            nc.vector.tensor_copy(got[:], word_table[:].bitcast(U32).indirect(lst[:]))
+            return got
+
+        def deal(src, dtype, name):
+            dealt = new([P, C], dtype, name)
+            nc.vector.tensor_copy(dealt[:].rearrange("p (t m) -> p m t", t=PACK), src[:].rearrange("p (m t) -> p m t", t=PACK))
+            return dealt
+
+        xq_scales = gather_scales(offs_sb, S, "xq_scales")
+        hc_scales = deal(gather_scales(hc_sb, C, "hc_scales_got"), U8, "hc_scales")
+        for r in range(2):
+            nc.sync.dma_start(hc_scales[2 + r:P:32, :].bitcast(I32), hc_scales[16 + r:P:32, :].bitcast(I32))
+
+        w_bf = new([P, PACK * H], BF16, "w_bf")
+        w_out = w_bf[:].rearrange("p (t m j) -> p m j t", t=PACK, j=PACK)
+        w_in = w_raw[:].rearrange("p j (m t) -> p m j t", t=PACK)
+        split = 64
+        nc.vector.tensor_copy(w_out[:, :split], w_in[:, :split])
+        nc.scalar.copy(w_out[:, split:], w_in[:, split:])
+        w_codes = new([P, H], U32, "w_codes")
+        w_scales = new([P, H], U8, "w_scales")
+        nc.vector.quantize_mx(out=w_codes[:].bitcast(FP8X4), scales=w_scales[:], in_=w_bf[:])
+
+        xq_words = gather_words(offs_sb, S, "xq_words")
+
+        def product(b, codes, scales, t, rhs, rhs_scales):
+            acc = bank(b)
+            cols = slice(t * P, (t + 1) * P)
+            nc.tensor.matmul_mx(out=acc[:], lhsT=codes[:, cols].bitcast(FP8X4), lhsT_scale=scales[:, cols],
+                                rhs=rhs[:].bitcast(FP8X4), rhs_scale=rhs_scales[:], start=True, stop=True)
+            return acc
+
+        y = []
+        for t in range(PACK):
+            acc = product(t, w_codes, w_scales, t, xq_words, xq_scales)
+            y_t = new([P, S], F32, "y%d" % t)
+            if t == 0:
+                nc.scalar.copy(y_t[:], acc[:])
+            else:
+                nc.vector.tensor_copy(y_t[:], acc[:])
+            y.append(y_t)
+
+        radicand, rb = [], []
+        for t in range(PACK):
+            pair = new([P, 2 * W], F32, "pair%d" % t)
+            nc.scalar.activation(pair[:, :W], y[t][:].indirect(n1_sb[:]), ACT.Copy)
+            nc.scalar.activation(pair[:, W:], y[t][:].indirect(n2_sb[:]), ACT.Copy)
+            rb_t = new([P, W], F32, "rb%d" % t)
+            nc.vector.scalar_tensor_tensor(rb_t[:], pair[:, :W], -0.5, pair[:, W:], ALU.mult, ALU.add)
+            squares = new([P, 2 * W], F32, "squares%d" % t)
+            nc.vector.tensor_tensor(squares[:], pair[:], pair[:], ALU.mult)
+            rad_t = new([P, W], F32, "radicand%d" % t)
+            nc.vector.scalar_tensor_tensor(rad_t[:], squares[:, :W], 0.25, squares[:, W:], ALU.add, ALU.add)
+            radicand.append(rad_t)
+            rb.append(rb_t)
+
+        z_bf = new([P, S * PACK], BF16, "z_bf")
+        z_slots = z_bf[:].rearrange("p (c t) -> p t c", t=PACK)
+        dt, ra = [], []
+
+        def finish_dt(t, pieces):
+            nc.scalar.activation(dt[t][:].indirect(n1_sb[:]), ra[t][:], ACT.Copy)
+            width = S // pieces
+            for u in range(pieces):
+                cols = slice(u * width, (u + 1) * width)
+                nc.vector.tensor_scalar(z_slots[:, t, cols], dt[t][:, cols], gs_sb[:, t:t + 1], None, ALU.mult)
+
+        for t in range(PACK):
+            dt.append(new([P, S], F32, "dt%d" % t))
+            nc.scalar.activation(dt[t][:].indirect(n2_sb[:]), rb[t][:], ACT.Copy)
+            ra.append(new([P, W], F32, "ra%d" % t))
+            nc.scalar.activation(ra[t][:], radicand[t][:], ACT.Sqrt)
+            if t > 0:
+                finish_dt(t - 1, 1)
+        finish_dt(PACK - 1, 2)
+
+        hc_words = deal(gather_words(hc_sb, C, "hc_words_got", "squares3"), U32, "hc_words")
+        ca_scales = deal(gather_scales(ca_sb, C, "ca_scales_got", "pair3"), U8, "ca_scales")
+        ca_words = deal(gather_words(ca_sb, C, "ca_words_got", "y3"), U32, "ca_words")
+
+        z_codes = new([P, S], U32, "z_codes")
+        z_scales = new([P, S], U8, "z_scales")
+        for u in range(2):
+            cols = slice(u * W, (u + 1) * W)
+            nc.vector.quantize_mx(out=z_codes[:, cols].bitcast(FP8X4), scales=z_scales[:, cols],
+                                  in_=z_bf[:, u * W * PACK:(u + 1) * W * PACK])
+
+        b_acc = [product(4 + t, hc_words, hc_scales, t, z_codes, z_scales) for t in range(PACK)]
+        a_acc = [product(t, ca_words, ca_scales, t, z_codes, z_scales) for t in range(PACK)]
+        out_rows = out.rearrange("(p t) c -> p t c", t=PACK)
+
+        a_win, b_win = {}, {}
+
+        def b_out(t):
+            b_win[t] = new([P, 2 * S], F32, "b_win%d" % t)
+            nc.scalar.activation(b_win[t][:, S:], b_acc[t][:], ACT.Tanh, scale=0.0625)
+            nc.vector.tensor_scalar(b_win[t][:, :S], b_acc[t][:], 0.0625, None, ALU.mult)
+
+        def b_side(t):
+            a_win[t] = new([P, 2 * S], F32, "a_win%d" % t)
+            nc.vector.tensor_scalar(a_win[t][:, :S], a_acc[t][:], 0.0625, None, ALU.mult)
+            gb = new([P, S], F32, "gb%d" % t)
+            nc.scalar.activation(gb[:], b_win[t][:].indirect(n4_sb[:]), ACT.Copy)
+            nc.vector.tensor_tensor(a_win[t][:, S:], b_win[t][:, S:], gb[:], ALU.mult)
+
+        def a_side(t, pieces):
+            width = S // pieces
+            for u in range(pieces):
+                cols = slice(u * width, (u + 1) * width)
+                ga = new([P, width], F32, "ga%d_%d" % (t, u))
+                nc.scalar.activation(ga[:], a_win[t][:].indirect(n3_sb[:, u * width // 16:(u + 1) * width // 16]), ACT.Copy)
+                res = new([P, width], F32, "res%d_%d" % (t, u))
+                nc.vector.tensor_tensor(res[:], ga[:], a_win[t][:, S + u * width:S + (u + 1) * width], ALU.subtract)
+                nc.sync.dma_start(out_rows[:, t, cols], res[:])
+
+        b_out(0)
+        for t in range(PACK):
+            if t + 1 < PACK:
+                b_out(t + 1)
+            b_side(t)
+            if t > 0:
+                a_side(t - 1, 1)
+        a_side(PACK - 1, 2)

@@ -37,19 +37,24 @@ def tile_picked_cdhsoftbpolar_none_p_kernel(tc, x_words, x_scales, w1, gs, offs,
             return psum.tile([P, S], F32, name="bank%d" % b)
 
         scale_table = new([P, T], U8, "scale_table")
-        nc.vector.memset(scale_table[:].bitcast(I32), 0)
-        rows = x_scales[0].bitcast(I32)
-        for r, step in ((0, 2), (1, 2), (2, 4), (3, 4)):
-            nc.scalar.dma_start(scale_table[r:P:8 * step, :].bitcast(I32), rows[r:16:step, :])
-        offs_sb = load_list(offs, "offs_sb")
-        hc_sb = load_list(hc, "hc_sb")
-        ca_sb = load_list(ca, "ca_sb")
+        nc.vector.memset(scale_table[:, :T // 2].bitcast(I32), 0)
+        nc.gpsimd.memset(scale_table[:, T // 2:].bitcast(I32), 0)
         w_raw = new([P, PACK, H], F32, "w_raw")
         nc.sync.dma_start(w_raw[:], w1.rearrange("(p j) c -> p j c", j=PACK))
+        offs_sb = load_list(offs, "offs_sb")
+        rows = x_scales[0].bitcast(I32)
+        for r, step, queue in ((0, 2, nc.scalar), (1, 2, nc.scalar), (2, 4, nc.sync), (3, 4, nc.sync)):
+            queue.dma_start(scale_table[r:P:8 * step, :].bitcast(I32), rows[r:16:step, :])
+        hc_sb = load_list(hc, "hc_sb")
         word_table = new([P, T], I32, "word_table")
         nc.sync.dma_start(word_table[:], x_words[0].rearrange("p c r -> p (c r)").bitcast(I32))
+        warm = new([P, 1], F32, "warm")
+        nc.vector.memset(warm[:], 1.0)
+        warm_out = new([P, 1], F32, "warm_out")
+        nc.scalar.activation(warm_out[:], warm[:], ACT.Sqrt)
         n1_sb = load_list(n1, "n1_sb")
         n2_sb = load_list(n2, "n2_sb")
+        ca_sb = load_list(ca, "ca_sb")
         gs_sb = new([P, PACK], F32, "gs_sb")
         nc.sync.dma_start(gs_sb[:], gs.rearrange("(p j) o -> p (j o)", j=PACK))
         n3_sb = load_list(n3, "n3_sb")
@@ -65,25 +70,26 @@ def tile_picked_cdhsoftbpolar_none_p_kernel(tc, x_words, x_scales, w1, gs, offs,
             nc.vector.tensor_copy(got[:], word_table[:].bitcast(U32).indirect(lst[:]))
             return got
 
-        def deal(src, dtype, name):
-            dealt = new([P, C], dtype, name)
+        def deal(src, dtype, name, tag=None):
+            dealt = new([P, C], dtype, name, tag)
             nc.vector.tensor_copy(dealt[:].rearrange("p (t m) -> p m t", t=PACK), src[:].rearrange("p (m t) -> p m t", t=PACK))
             return dealt
 
-        xq_scales = gather_scales(offs_sb, S, "xq_scales")
-        hc_scales = deal(gather_scales(hc_sb, C, "hc_scales_got"), U8, "hc_scales")
-        for r in range(2):
-            nc.sync.dma_start(hc_scales[2 + r:P:32, :].bitcast(I32), hc_scales[16 + r:P:32, :].bitcast(I32))
 
         w_bf = new([P, PACK * H], BF16, "w_bf")
         w_out = w_bf[:].rearrange("p (t m j) -> p m j t", t=PACK, j=PACK)
         w_in = w_raw[:].rearrange("p j (m t) -> p m j t", t=PACK)
-        split = 64
+        split = 56
         nc.vector.tensor_copy(w_out[:, :split], w_in[:, :split])
         nc.scalar.copy(w_out[:, split:], w_in[:, split:])
+        xq_scales = gather_scales(offs_sb, S, "xq_scales")
         w_codes = new([P, H], U32, "w_codes")
         w_scales = new([P, H], U8, "w_scales")
         nc.vector.quantize_mx(out=w_codes[:].bitcast(FP8X4), scales=w_scales[:], in_=w_bf[:])
+
+        half = C // 2
+        hc_scales_got = new([P, half], U8, "hc_scales_got")
+        nc.vector.tensor_copy(hc_scales_got[:], scale_table[:].indirect(hc_sb[:, :half // 16]))
 
         xq_words = gather_words(offs_sb, S, "xq_words")
 
@@ -104,44 +110,51 @@ def tile_picked_cdhsoftbpolar_none_p_kernel(tc, x_words, x_scales, w1, gs, offs,
                 nc.vector.tensor_copy(y_t[:], acc[:])
             y.append(y_t)
 
-        radicand, rb = [], []
+        rb, a_win = [], []
+        radicand = new([P, PACK * W], F32, "radicand")
         for t in range(PACK):
-            pair = new([P, 2 * W], F32, "pair%d" % t)
+            a_win.append(new([P, 2 * S], F32, "a_win%d" % t))
+            pair = a_win[t][:, S:]
             nc.scalar.activation(pair[:, :W], y[t][:].indirect(n1_sb[:]), ACT.Copy)
             nc.scalar.activation(pair[:, W:], y[t][:].indirect(n2_sb[:]), ACT.Copy)
-            rb_t = new([P, W], F32, "rb%d" % t)
-            nc.vector.scalar_tensor_tensor(rb_t[:], pair[:, :W], -0.5, pair[:, W:], ALU.mult, ALU.add)
             squares = new([P, 2 * W], F32, "squares%d" % t)
-            nc.vector.tensor_tensor(squares[:], pair[:], pair[:], ALU.mult)
-            rad_t = new([P, W], F32, "radicand%d" % t)
-            nc.vector.scalar_tensor_tensor(rad_t[:], squares[:, :W], 0.25, squares[:, W:], ALU.add, ALU.add)
-            radicand.append(rad_t)
-            rb.append(rb_t)
+            rb.append(new([P, W], F32, "rb%d" % t))
+            if t < PACK - 1:
+                nc.vector.scalar_tensor_tensor(rb[t][:], pair[:, :W], -0.5, pair[:, W:], ALU.mult, ALU.add)
+            nc.vector.tensor_tensor(squares[:], pair, pair, ALU.mult)
+            nc.vector.scalar_tensor_tensor(radicand[:, t * W:(t + 1) * W], squares[:, :W], 0.25, squares[:, W:], ALU.add, ALU.add)
+            if t == PACK - 1:
+                nc.vector.scalar_tensor_tensor(rb[t][:], pair[:, :W], -0.5, pair[:, W:], ALU.mult, ALU.add)
 
+        hc_scales_rest = new([P, half], U8, "hc_scales_rest", "y2")
+        nc.vector.tensor_copy(hc_scales_rest[:], scale_table[:].indirect(hc_sb[:, half // 16:]))
+        hc_scales = new([P, C], U8, "hc_scales")
+        for u, got in enumerate((hc_scales_got, hc_scales_rest)):
+            nc.vector.tensor_copy(hc_scales[:].rearrange("p (t m) -> p m t", t=PACK)[:, u * half // PACK:(u + 1) * half // PACK],
+                                  got[:].rearrange("p (m t) -> p m t", t=PACK))
+        for r in range(2):
+            nc.sync.dma_start(hc_scales[2 + r:P:32, :].bitcast(I32), hc_scales[16 + r:P:32, :].bitcast(I32))
+        hc_words = deal(gather_words(hc_sb, C, "hc_words_got", "squares3"), U32, "hc_words")
+        ca_words = deal(gather_words(ca_sb, C, "ca_words_got", "squares2"), U32, "ca_words")
+        ca_scales = deal(gather_scales(ca_sb, C, "ca_scales_got", "y3"), U8, "ca_scales")
+
+        ra = new([P, PACK * W], F32, "ra")
+        nc.scalar.activation(ra[:], radicand[:], ACT.Sqrt)
+        dt = [new([P, S], F32, "dt%d" % t) for t in range(PACK)]
+        for t in range(PACK):
+            nc.scalar.activation(dt[t][:].indirect(n2_sb[:]), rb[t][:], ACT.Copy)
         z_bf = new([P, S * PACK], BF16, "z_bf")
         z_slots = z_bf[:].rearrange("p (c t) -> p t c", t=PACK)
-        dt, ra = [], []
-
-        def finish_dt(t, pieces):
-            nc.scalar.activation(dt[t][:].indirect(n1_sb[:]), ra[t][:], ACT.Copy)
+        for t in range(PACK):
+            nc.scalar.activation(dt[t][:].indirect(n1_sb[:]), ra[:, t * W:(t + 1) * W], ACT.Copy)
+            pieces = 2 if t == PACK - 1 else 1
             width = S // pieces
             for u in range(pieces):
                 cols = slice(u * width, (u + 1) * width)
                 nc.vector.tensor_scalar(z_slots[:, t, cols], dt[t][:, cols], gs_sb[:, t:t + 1], None, ALU.mult)
 
-        for t in range(PACK):
-            dt.append(new([P, S], F32, "dt%d" % t))
-            nc.scalar.activation(dt[t][:].indirect(n2_sb[:]), rb[t][:], ACT.Copy)
-            ra.append(new([P, W], F32, "ra%d" % t))
-            nc.scalar.activation(ra[t][:], radicand[t][:], ACT.Sqrt)
-            if t > 0:
-                finish_dt(t - 1, 1)
-        finish_dt(PACK - 1, 2)
-
-        hc_words = deal(gather_words(hc_sb, C, "hc_words_got", "squares3"), U32, "hc_words")
-        ca_scales = deal(gather_scales(ca_sb, C, "ca_scales_got", "pair3"), U8, "ca_scales")
-        ca_words = deal(gather_words(ca_sb, C, "ca_words_got", "y3"), U32, "ca_words")
-
+        warm_tanh = new([P, 1], F32, "warm_tanh")
+        nc.scalar.activation(warm_tanh[:], dt[PACK - 1][:, :1], ACT.Tanh)
         z_codes = new([P, S], U32, "z_codes")
         z_scales = new([P, S], U8, "z_scales")
         for u in range(2):
@@ -153,35 +166,36 @@ def tile_picked_cdhsoftbpolar_none_p_kernel(tc, x_words, x_scales, w1, gs, offs,
         a_acc = [product(t, ca_words, ca_scales, t, z_codes, z_scales) for t in range(PACK)]
         out_rows = out.rearrange("(p t) c -> p t c", t=PACK)
 
-        a_win, b_win = {}, {}
+        b_win, ga, damped = {}, {}, {}
 
-        def b_out(t):
+        for t in range(PACK):
             b_win[t] = new([P, 2 * S], F32, "b_win%d" % t)
             nc.scalar.activation(b_win[t][:, S:], b_acc[t][:], ACT.Tanh, scale=0.0625)
             nc.vector.tensor_scalar(b_win[t][:, :S], b_acc[t][:], 0.0625, None, ALU.mult)
-
-        def b_side(t):
-            a_win[t] = new([P, 2 * S], F32, "a_win%d" % t)
+        for t in range(PACK):
             nc.vector.tensor_scalar(a_win[t][:, :S], a_acc[t][:], 0.0625, None, ALU.mult)
+
+        def fetch_b(t):
             gb = new([P, S], F32, "gb%d" % t)
             nc.scalar.activation(gb[:], b_win[t][:].indirect(n4_sb[:]), ACT.Copy)
-            nc.vector.tensor_tensor(a_win[t][:, S:], b_win[t][:, S:], gb[:], ALU.mult)
+            damped[t] = new([P, S], F32, "damped%d" % t)
+            nc.vector.tensor_tensor(damped[t][:], b_win[t][:, S:], gb[:], ALU.mult)
 
-        def a_side(t, pieces):
-            width = S // pieces
-            for u in range(pieces):
-                cols = slice(u * width, (u + 1) * width)
-                ga = new([P, width], F32, "ga%d_%d" % (t, u))
-                nc.scalar.activation(ga[:], a_win[t][:].indirect(n3_sb[:, u * width // 16:(u + 1) * width // 16]), ACT.Copy)
-                res = new([P, width], F32, "res%d_%d" % (t, u))
-                nc.vector.tensor_tensor(res[:], ga[:], a_win[t][:, S + u * width:S + (u + 1) * width], ALU.subtract)
-                nc.sync.dma_start(out_rows[:, t, cols], res[:])
+        def fetch_a(t, u, width):
+            ga[t, u] = new([P, width], F32, "ga%d_%d" % (t, u))
+            nc.scalar.activation(ga[t, u][:], a_win[t][:].indirect(n3_sb[:, u * width // 16:(u + 1) * width // 16]), ACT.Copy)
 
-        b_out(0)
+        def finish(t, u, width):
+            cols = slice(u * width, (u + 1) * width)
+            res = new([P, width], F32, "res%d_%d" % (t, u))
+            nc.vector.tensor_tensor(res[:], ga[t, u][:], damped[t][:, cols], ALU.subtract)
+            nc.sync.dma_start(out_rows[:, t, cols], res[:])
+
+        fetch_b(0)
         for t in range(PACK):
             if t + 1 < PACK:
-                b_out(t + 1)
-            b_side(t)
-            if t > 0:
-                a_side(t - 1, 1)
-        a_side(PACK - 1, 2)
+                fetch_b(t + 1)
+            pieces = 2 if t == PACK - 1 else 1
+            for u in range(pieces):
+                fetch_a(t, u, S // pieces)
+                finish(t, u, S // pieces)

@@ -39,9 +39,9 @@ def tile_picked_cdhsoftbpolar_none_p_kernel(tc, x_words, x_scales, w1, gs, offs,
         scale_table = new([P, T], U8, "scale_table")
         nc.vector.memset(scale_table[:, :T // 2].bitcast(I32), 0)
         nc.gpsimd.memset(scale_table[:, T // 2:].bitcast(I32), 0)
+        offs_sb = load_list(offs, "offs_sb")
         w_raw = new([P, PACK, H], F32, "w_raw")
         nc.sync.dma_start(w_raw[:], w1.rearrange("(p j) c -> p j c", j=PACK))
-        offs_sb = load_list(offs, "offs_sb")
         rows = x_scales[0].bitcast(I32)
         for r, step, queue in ((0, 2, nc.scalar), (1, 2, nc.scalar), (2, 4, nc.sync), (3, 4, nc.sync)):
             queue.dma_start(scale_table[r:P:8 * step, :].bitcast(I32), rows[r:16:step, :])
@@ -79,7 +79,7 @@ def tile_picked_cdhsoftbpolar_none_p_kernel(tc, x_words, x_scales, w1, gs, offs,
         w_bf = new([P, PACK * H], BF16, "w_bf")
         w_out = w_bf[:].rearrange("p (t m j) -> p m j t", t=PACK, j=PACK)
         w_in = w_raw[:].rearrange("p j (m t) -> p m j t", t=PACK)
-        split = 56
+        split = 64
         nc.vector.tensor_copy(w_out[:, :split], w_in[:, :split])
         nc.scalar.copy(w_out[:, split:], w_in[:, split:])
         xq_scales = gather_scales(offs_sb, S, "xq_scales")
@@ -87,11 +87,8 @@ def tile_picked_cdhsoftbpolar_none_p_kernel(tc, x_words, x_scales, w1, gs, offs,
         w_scales = new([P, H], U8, "w_scales")
         nc.vector.quantize_mx(out=w_codes[:].bitcast(FP8X4), scales=w_scales[:], in_=w_bf[:])
 
-        half = C // 2
-        hc_scales_got = new([P, half], U8, "hc_scales_got")
-        nc.vector.tensor_copy(hc_scales_got[:], scale_table[:].indirect(hc_sb[:, :half // 16]))
-
         xq_words = gather_words(offs_sb, S, "xq_words")
+        hc_words_got = gather_words(hc_sb, C, "hc_words_got")
 
         def product(b, codes, scales, t, rhs, rhs_scales):
             acc = bank(b)
@@ -126,15 +123,10 @@ def tile_picked_cdhsoftbpolar_none_p_kernel(tc, x_words, x_scales, w1, gs, offs,
             if t == PACK - 1:
                 nc.vector.scalar_tensor_tensor(rb[t][:], pair[:, :W], -0.5, pair[:, W:], ALU.mult, ALU.add)
 
-        hc_scales_rest = new([P, half], U8, "hc_scales_rest", "y2")
-        nc.vector.tensor_copy(hc_scales_rest[:], scale_table[:].indirect(hc_sb[:, half // 16:]))
-        hc_scales = new([P, C], U8, "hc_scales")
-        for u, got in enumerate((hc_scales_got, hc_scales_rest)):
-            nc.vector.tensor_copy(hc_scales[:].rearrange("p (t m) -> p m t", t=PACK)[:, u * half // PACK:(u + 1) * half // PACK],
-                                  got[:].rearrange("p (m t) -> p m t", t=PACK))
+        hc_scales = deal(gather_scales(hc_sb, C, "hc_scales_got", "y2"), U8, "hc_scales")
         for r in range(2):
             nc.sync.dma_start(hc_scales[2 + r:P:32, :].bitcast(I32), hc_scales[16 + r:P:32, :].bitcast(I32))
-        hc_words = deal(gather_words(hc_sb, C, "hc_words_got", "squares3"), U32, "hc_words")
+        hc_words = deal(hc_words_got, U32, "hc_words", "squares3")
         ca_words = deal(gather_words(ca_sb, C, "ca_words_got", "squares2"), U32, "ca_words")
         ca_scales = deal(gather_scales(ca_sb, C, "ca_scales_got", "y3"), U8, "ca_scales")
 
@@ -163,7 +155,6 @@ def tile_picked_cdhsoftbpolar_none_p_kernel(tc, x_words, x_scales, w1, gs, offs,
                                   in_=z_bf[:, u * W * PACK:(u + 1) * W * PACK])
 
         b_acc = [product(4 + t, hc_words, hc_scales, t, z_codes, z_scales) for t in range(PACK)]
-        a_acc = [product(t, ca_words, ca_scales, t, z_codes, z_scales) for t in range(PACK)]
         out_rows = out.rearrange("(p t) c -> p t c", t=PACK)
 
         b_win, ga, damped = {}, {}, {}
@@ -173,7 +164,8 @@ def tile_picked_cdhsoftbpolar_none_p_kernel(tc, x_words, x_scales, w1, gs, offs,
             nc.scalar.activation(b_win[t][:, S:], b_acc[t][:], ACT.Tanh, scale=0.0625)
             nc.vector.tensor_scalar(b_win[t][:, :S], b_acc[t][:], 0.0625, None, ALU.mult)
         for t in range(PACK):
-            nc.vector.tensor_scalar(a_win[t][:, :S], a_acc[t][:], 0.0625, None, ALU.mult)
+            a_acc = product(4 + t, ca_words, ca_scales, t, z_codes, z_scales)
+            nc.vector.tensor_scalar(a_win[t][:, :S], a_acc[:], 0.0625, None, ALU.mult)
 
         def fetch_b(t):
             gb = new([P, S], F32, "gb%d" % t)

@@ -17,6 +17,12 @@ ACT = mybir.ActivationFunctionType
 
 P = 128
 PACK = 4
+LAST = PACK - 1
+GROUP = 16
+QUADRANT = 32
+SCALE_ROWS = K // 32
+SCORE_SCALE = 0.0625
+CAST_SPLIT = P // 2
 
 
 def tile_picked_cdhsoftbpolar_none_p_kernel(tc, x_words, x_scales, w1, gs, offs, n1, n2, ca, hc, n3, n4, out):
@@ -25,16 +31,17 @@ def tile_picked_cdhsoftbpolar_none_p_kernel(tc, x_words, x_scales, w1, gs, offs,
         keep = ctx.enter_context(tc.tile_pool(name="keep", bufs=1))
         psum = ctx.enter_context(tc.psum_pool(name="psum", bufs=1))
 
-        def new(shape, dtype, name, tag=None):
-            return keep.tile(shape, dtype, name=name, tag=tag or name, align_bytes=64)
+        def new(shape, dtype, name, reuse=None):
+            return keep.tile(shape, dtype, name=name, tag=reuse or name, align_bytes=64)
 
         def load_list(src, name):
             held = new(list(src.shape), U16, name)
             nc.sync.dma_start(held[:], src)
             return held
 
-        def bank(b):
-            return psum.tile([P, S], F32, name="bank%d" % b)
+        def spans(pieces):
+            width = S // pieces
+            return [slice(u * width, (u + 1) * width) for u in range(pieces)]
 
         scale_table = new([P, T], U8, "scale_table")
         nc.vector.memset(scale_table[:, :T // 2].bitcast(I32), 0)
@@ -42,16 +49,20 @@ def tile_picked_cdhsoftbpolar_none_p_kernel(tc, x_words, x_scales, w1, gs, offs,
         offs_sb = load_list(offs, "offs_sb")
         w_raw = new([P, PACK, H], F32, "w_raw")
         nc.sync.dma_start(w_raw[:], w1.rearrange("(p j) c -> p j c", j=PACK))
-        rows = x_scales[0].bitcast(I32)
-        for r, step, queue in ((0, 2, nc.scalar), (1, 2, nc.scalar), (2, 4, nc.sync), (3, 4, nc.sync)):
-            queue.dma_start(scale_table[r:P:8 * step, :].bitcast(I32), rows[r:16:step, :])
+        scale_rows = x_scales[0].bitcast(I32)
+        for r in range(2):
+            nc.scalar.dma_start(scale_table[r:P:GROUP, :].bitcast(I32), scale_rows[r:SCALE_ROWS:2, :])
+        for r in range(2, PACK):
+            nc.sync.dma_start(scale_table[r:P:QUADRANT, :].bitcast(I32), scale_rows[r:SCALE_ROWS:PACK, :])
         hc_sb = load_list(hc, "hc_sb")
         word_table = new([P, T], I32, "word_table")
         nc.sync.dma_start(word_table[:], x_words[0].rearrange("p c r -> p (c r)").bitcast(I32))
-        warm = new([P, 1], F32, "warm")
-        nc.vector.memset(warm[:], 1.0)
-        warm_out = new([P, 1], F32, "warm_out")
-        nc.scalar.activation(warm_out[:], warm[:], ACT.Sqrt)
+
+        sqrt_warm_in = new([P, 1], F32, "sqrt_warm_in")
+        nc.vector.memset(sqrt_warm_in[:], 1.0)
+        sqrt_warm_out = new([P, 1], F32, "sqrt_warm_out")
+        nc.scalar.activation(sqrt_warm_out[:], sqrt_warm_in[:], ACT.Sqrt)
+
         n1_sb = load_list(n1, "n1_sb")
         n2_sb = load_list(n2, "n2_sb")
         ca_sb = load_list(ca, "ca_sb")
@@ -60,74 +71,71 @@ def tile_picked_cdhsoftbpolar_none_p_kernel(tc, x_words, x_scales, w1, gs, offs,
         n3_sb = load_list(n3, "n3_sb")
         n4_sb = load_list(n4, "n4_sb")
 
-        def gather_scales(lst, n, name, tag=None):
-            got = new([P, n], U8, name, tag)
-            nc.vector.tensor_copy(got[:], scale_table[:].indirect(lst[:]))
+        def gather_scales(offsets, n, name, reuse=None):
+            got = new([P, n], U8, name, reuse)
+            nc.vector.tensor_copy(got[:], scale_table[:].indirect(offsets[:]))
             return got
 
-        def gather_words(lst, n, name, tag=None):
-            got = new([P, n], U32, name, tag)
-            nc.vector.tensor_copy(got[:], word_table[:].bitcast(U32).indirect(lst[:]))
+        def gather_words(offsets, n, name, reuse=None):
+            got = new([P, n], U32, name, reuse)
+            nc.vector.tensor_copy(got[:], word_table[:].bitcast(U32).indirect(offsets[:]))
             return got
 
-        def deal(src, dtype, name, tag=None):
-            dealt = new([P, C], dtype, name, tag)
+        def deal(src, dtype, name):
+            dealt = new([P, C], dtype, name)
             nc.vector.tensor_copy(dealt[:].rearrange("p (t m) -> p m t", t=PACK), src[:].rearrange("p (m t) -> p m t", t=PACK))
             return dealt
 
+        def product(bank, codes, scales, t, rhs, rhs_scales):
+            acc = psum.tile([P, rhs.shape[1]], F32, name="bank%d" % bank)
+            cols = slice(t * P, (t + 1) * P)
+            nc.tensor.matmul_mx(out=acc[:], lhsT=codes[:, cols].bitcast(FP8X4), lhsT_scale=scales[:, cols],
+                                rhs=rhs.bitcast(FP8X4), rhs_scale=rhs_scales, start=True, stop=True)
+            return acc
 
         w_bf = new([P, PACK * H], BF16, "w_bf")
         w_out = w_bf[:].rearrange("p (t m j) -> p m j t", t=PACK, j=PACK)
         w_in = w_raw[:].rearrange("p j (m t) -> p m j t", t=PACK)
-        split = 64
-        nc.vector.tensor_copy(w_out[:, :split], w_in[:, :split])
-        nc.scalar.copy(w_out[:, split:], w_in[:, split:])
+        nc.vector.tensor_copy(w_out[:, :CAST_SPLIT], w_in[:, :CAST_SPLIT])
+        nc.scalar.copy(w_out[:, CAST_SPLIT:], w_in[:, CAST_SPLIT:])
         xq_scales = gather_scales(offs_sb, S, "xq_scales")
         w_codes = new([P, H], U32, "w_codes")
         w_scales = new([P, H], U8, "w_scales")
         nc.vector.quantize_mx(out=w_codes[:].bitcast(FP8X4), scales=w_scales[:], in_=w_bf[:])
 
         xq_words = gather_words(offs_sb, S, "xq_words")
-        hc_words_got = gather_words(hc_sb, C, "hc_words_got")
-
-        def product(b, codes, scales, t, rhs, rhs_scales):
-            acc = bank(b)
-            cols = slice(t * P, (t + 1) * P)
-            nc.tensor.matmul_mx(out=acc[:], lhsT=codes[:, cols].bitcast(FP8X4), lhsT_scale=scales[:, cols],
-                                rhs=rhs[:].bitcast(FP8X4), rhs_scale=rhs_scales[:], start=True, stop=True)
-            return acc
+        hc_words = deal(gather_words(hc_sb, C, "hc_words_got"), U32, "hc_words")
 
         y = []
         for t in range(PACK):
-            acc = product(t, w_codes, w_scales, t, xq_words, xq_scales)
-            y_t = new([P, S], F32, "y%d" % t)
+            y_acc = product(t, w_codes, w_scales, t, xq_words[:], xq_scales[:])
+            y.append(new([P, S], F32, "y%d" % t))
             if t == 0:
-                nc.scalar.copy(y_t[:], acc[:])
+                nc.scalar.copy(y[t][:], y_acc[:])
             else:
-                nc.vector.tensor_copy(y_t[:], acc[:])
-            y.append(y_t)
+                nc.vector.tensor_copy(y[t][:], y_acc[:])
 
         rb, a_win = [], []
         radicand = new([P, PACK * W], F32, "radicand")
         for t in range(PACK):
             a_win.append(new([P, 2 * S], F32, "a_win%d" % t))
             pair = a_win[t][:, S:]
-            nc.scalar.activation(pair[:, :W], y[t][:].indirect(n1_sb[:]), ACT.Copy)
-            nc.scalar.activation(pair[:, W:], y[t][:].indirect(n2_sb[:]), ACT.Copy)
+            pa, pb = pair[:, :W], pair[:, W:]
+            nc.scalar.activation(pa, y[t][:].indirect(n1_sb[:]), ACT.Copy)
+            nc.scalar.activation(pb, y[t][:].indirect(n2_sb[:]), ACT.Copy)
             squares = new([P, 2 * W], F32, "squares%d" % t)
             rb.append(new([P, W], F32, "rb%d" % t))
-            if t < PACK - 1:
-                nc.vector.scalar_tensor_tensor(rb[t][:], pair[:, :W], -0.5, pair[:, W:], ALU.mult, ALU.add)
+            if t < LAST:
+                nc.vector.scalar_tensor_tensor(rb[t][:], pa, -0.5, pb, ALU.mult, ALU.add)
             nc.vector.tensor_tensor(squares[:], pair, pair, ALU.mult)
             nc.vector.scalar_tensor_tensor(radicand[:, t * W:(t + 1) * W], squares[:, :W], 0.25, squares[:, W:], ALU.add, ALU.add)
-            if t == PACK - 1:
-                nc.vector.scalar_tensor_tensor(rb[t][:], pair[:, :W], -0.5, pair[:, W:], ALU.mult, ALU.add)
+            if t == LAST:
+                nc.vector.scalar_tensor_tensor(rb[t][:], pa, -0.5, pb, ALU.mult, ALU.add)
 
         hc_scales = deal(gather_scales(hc_sb, C, "hc_scales_got", "y2"), U8, "hc_scales")
         for r in range(2):
-            nc.sync.dma_start(hc_scales[2 + r:P:32, :].bitcast(I32), hc_scales[16 + r:P:32, :].bitcast(I32))
-        hc_words = deal(hc_words_got, U32, "hc_words", "squares3")
-        ca_words = deal(gather_words(ca_sb, C, "ca_words_got", "squares2"), U32, "ca_words")
+            nc.sync.dma_start(hc_scales[2 + r:P:QUADRANT, :].bitcast(I32), hc_scales[GROUP + r:P:QUADRANT, :].bitcast(I32))
+        ca_words = deal(gather_words(ca_sb, C, "ca_words_got", "squares3"), U32, "ca_words")
         ca_scales = deal(gather_scales(ca_sb, C, "ca_scales_got", "y3"), U8, "ca_scales")
 
         ra = new([P, PACK * W], F32, "ra")
@@ -139,55 +147,51 @@ def tile_picked_cdhsoftbpolar_none_p_kernel(tc, x_words, x_scales, w1, gs, offs,
         z_slots = z_bf[:].rearrange("p (c t) -> p t c", t=PACK)
         for t in range(PACK):
             nc.scalar.activation(dt[t][:].indirect(n1_sb[:]), ra[:, t * W:(t + 1) * W], ACT.Copy)
-            pieces = 2 if t == PACK - 1 else 1
-            width = S // pieces
-            for u in range(pieces):
-                cols = slice(u * width, (u + 1) * width)
+            for cols in spans(2 if t == LAST else 1):
                 nc.vector.tensor_scalar(z_slots[:, t, cols], dt[t][:, cols], gs_sb[:, t:t + 1], None, ALU.mult)
 
-        warm_tanh = new([P, 1], F32, "warm_tanh")
-        nc.scalar.activation(warm_tanh[:], dt[PACK - 1][:, :1], ACT.Tanh)
+        tanh_warm_out = new([P, 1], F32, "tanh_warm_out")
+        nc.scalar.activation(tanh_warm_out[:], dt[LAST - 1][:, :1], ACT.Tanh)
+
         z_codes = new([P, S], U32, "z_codes")
         z_scales = new([P, S], U8, "z_scales")
-        for u in range(2):
-            cols = slice(u * W, (u + 1) * W)
+        for cols in spans(2):
             nc.vector.quantize_mx(out=z_codes[:, cols].bitcast(FP8X4), scales=z_scales[:, cols],
-                                  in_=z_bf[:, u * W * PACK:(u + 1) * W * PACK])
+                                  in_=z_bf[:, cols.start * PACK:cols.stop * PACK])
 
-        b_acc = [product(4 + t, hc_words, hc_scales, t, z_codes, z_scales) for t in range(PACK)]
+        b_win = []
+        for t in range(PACK):
+            b_win.append(new([P, 2 * S], F32, "b_win%d" % t))
+            for cols in spans(2 if t == 0 else 1):
+                bank = PACK + t if cols.stop == S else 0
+                b_acc = product(bank, hc_words, hc_scales, t, z_codes[:, cols], z_scales[:, cols])
+                nc.scalar.activation(b_win[t][:, S:][:, cols], b_acc[:], ACT.Tanh, scale=SCORE_SCALE)
+                nc.vector.tensor_scalar(b_win[t][:, cols], b_acc[:], SCORE_SCALE, None, ALU.mult)
+        for t in range(PACK):
+            a_acc = product(PACK + t, ca_words, ca_scales, t, z_codes[:], z_scales[:])
+            nc.vector.tensor_scalar(a_win[t][:, :S], a_acc[:], SCORE_SCALE, None, ALU.mult)
+
         out_rows = out.rearrange("(p t) c -> p t c", t=PACK)
-
-        b_win, ga, damped = {}, {}, {}
-
-        for t in range(PACK):
-            b_win[t] = new([P, 2 * S], F32, "b_win%d" % t)
-            nc.scalar.activation(b_win[t][:, S:], b_acc[t][:], ACT.Tanh, scale=0.0625)
-            nc.vector.tensor_scalar(b_win[t][:, :S], b_acc[t][:], 0.0625, None, ALU.mult)
-        for t in range(PACK):
-            a_acc = product(4 + t, ca_words, ca_scales, t, z_codes, z_scales)
-            nc.vector.tensor_scalar(a_win[t][:, :S], a_acc[:], 0.0625, None, ALU.mult)
+        damped = []
 
         def fetch_b(t):
             gb = new([P, S], F32, "gb%d" % t)
             nc.scalar.activation(gb[:], b_win[t][:].indirect(n4_sb[:]), ACT.Copy)
-            damped[t] = new([P, S], F32, "damped%d" % t)
+            damped.append(new([P, S], F32, "damped%d" % t))
             nc.vector.tensor_tensor(damped[t][:], b_win[t][:, S:], gb[:], ALU.mult)
 
-        def fetch_a(t, u, width):
-            ga[t, u] = new([P, width], F32, "ga%d_%d" % (t, u))
-            nc.scalar.activation(ga[t, u][:], a_win[t][:].indirect(n3_sb[:, u * width // 16:(u + 1) * width // 16]), ACT.Copy)
-
-        def finish(t, u, width):
-            cols = slice(u * width, (u + 1) * width)
-            res = new([P, width], F32, "res%d_%d" % (t, u))
-            nc.vector.tensor_tensor(res[:], ga[t, u][:], damped[t][:, cols], ALU.subtract)
-            nc.sync.dma_start(out_rows[:, t, cols], res[:])
+        def fetch_a_and_store(t, cols):
+            width = cols.stop - cols.start
+            ga = new([P, width], F32, "ga%d_%d" % (t, cols.start))
+            offsets = n3_sb[:, cols.start // GROUP:cols.stop // GROUP]
+            nc.scalar.activation(ga[:], a_win[t][:].indirect(offsets), ACT.Copy)
+            result = new([P, width], F32, "result%d_%d" % (t, cols.start))
+            nc.vector.tensor_tensor(result[:], ga[:], damped[t][:, cols], ALU.subtract)
+            nc.sync.dma_start(out_rows[:, t, cols], result[:])
 
         fetch_b(0)
         for t in range(PACK):
-            if t + 1 < PACK:
+            if t < LAST:
                 fetch_b(t + 1)
-            pieces = 2 if t == PACK - 1 else 1
-            for u in range(pieces):
-                fetch_a(t, u, S // pieces)
-                finish(t, u, S // pieces)
+            for cols in spans(2 if t == LAST else 1):
+                fetch_a_and_store(t, cols)

from contextlib import ExitStack

import concourse.mybir as mybir

K, T, S, H, W, C = 512, 2048, 256, 512, 128, 512
FLOPS = 2 * K * H * S + 2 * 2 * K * C * S

F32 = mybir.dt.float32
BF16 = mybir.dt.bfloat16
I32 = mybir.dt.int32
U32 = mybir.dt.uint32
U16 = mybir.dt.uint16
U8 = mybir.dt.uint8
FP8X4 = mybir.dt.float8_e4m3fn_x4
ALU = mybir.AluOpType
ACT = mybir.ActivationFunctionType

P = 128
PACK = 4
LAST = PACK - 1
GROUP = 16
QUADRANT = 32
SCALE_ROWS = K // 32
SCORE_SCALE = 0.0625
CAST_SPLIT = P // 2


def tile_picked_cdhsoftbpolar_none_p_kernel(tc, x_words, x_scales, w1, gs, offs, n1, n2, ca, hc, n3, n4, out):
    nc = tc.nc
    with ExitStack() as ctx:
        keep = ctx.enter_context(tc.tile_pool(name="keep", bufs=1))
        psum = ctx.enter_context(tc.psum_pool(name="psum", bufs=1))

        def new(shape, dtype, name, reuse=None):
            return keep.tile(shape, dtype, name=name, tag=reuse or name, align_bytes=64)

        def load_list(src, name):
            held = new(list(src.shape), U16, name)
            nc.sync.dma_start(held[:], src)
            return held

        def spans(pieces):
            width = S // pieces
            return [slice(u * width, (u + 1) * width) for u in range(pieces)]

        scale_table = new([P, T], U8, "scale_table")
        nc.vector.memset(scale_table[:, :T // 2].bitcast(I32), 0)
        nc.gpsimd.memset(scale_table[:, T // 2:].bitcast(I32), 0)
        offs_sb = load_list(offs, "offs_sb")
        w_raw = new([P, PACK, H], F32, "w_raw")
        nc.sync.dma_start(w_raw[:], w1.rearrange("(p j) c -> p j c", j=PACK))
        scale_rows = x_scales[0].bitcast(I32)
        for r in range(2):
            nc.scalar.dma_start(scale_table[r:P:GROUP, :].bitcast(I32), scale_rows[r:SCALE_ROWS:2, :])
        for r in range(2, PACK):
            nc.sync.dma_start(scale_table[r:P:QUADRANT, :].bitcast(I32), scale_rows[r:SCALE_ROWS:PACK, :])
        hc_sb = load_list(hc, "hc_sb")
        word_table = new([P, T], I32, "word_table")
        nc.sync.dma_start(word_table[:], x_words[0].rearrange("p c r -> p (c r)").bitcast(I32))

        sqrt_warm_in = new([P, 1], F32, "sqrt_warm_in")
        nc.vector.memset(sqrt_warm_in[:], 1.0)
        sqrt_warm_out = new([P, 1], F32, "sqrt_warm_out")
        nc.scalar.activation(sqrt_warm_out[:], sqrt_warm_in[:], ACT.Sqrt)

        n1_sb = load_list(n1, "n1_sb")
        n2_sb = load_list(n2, "n2_sb")
        ca_sb = load_list(ca, "ca_sb")
        gs_sb = new([P, PACK], F32, "gs_sb")
        nc.sync.dma_start(gs_sb[:], gs.rearrange("(p j) o -> p (j o)", j=PACK))
        n3_sb = load_list(n3, "n3_sb")
        n4_sb = load_list(n4, "n4_sb")

        def gather_scales(offsets, n, name, reuse=None):
            got = new([P, n], U8, name, reuse)
            nc.vector.tensor_copy(got[:], scale_table[:].indirect(offsets[:]))
            return got

        def gather_words(offsets, n, name, reuse=None):
            got = new([P, n], U32, name, reuse)
            nc.vector.tensor_copy(got[:], word_table[:].bitcast(U32).indirect(offsets[:]))
            return got

        def deal(src, dtype, name):
            dealt = new([P, C], dtype, name)
            nc.vector.tensor_copy(dealt[:].rearrange("p (t m) -> p m t", t=PACK), src[:].rearrange("p (m t) -> p m t", t=PACK))
            return dealt

        def product(bank, codes, scales, t, rhs, rhs_scales):
            acc = psum.tile([P, rhs.shape[1]], F32, name="bank%d" % bank)
            cols = slice(t * P, (t + 1) * P)
            nc.tensor.matmul_mx(out=acc[:], lhsT=codes[:, cols].bitcast(FP8X4), lhsT_scale=scales[:, cols],
                                rhs=rhs.bitcast(FP8X4), rhs_scale=rhs_scales, start=True, stop=True)
            return acc

        w_bf = new([P, PACK * H], BF16, "w_bf")
        w_out = w_bf[:].rearrange("p (t m j) -> p m j t", t=PACK, j=PACK)
        w_in = w_raw[:].rearrange("p j (m t) -> p m j t", t=PACK)
        nc.vector.tensor_copy(w_out[:, :CAST_SPLIT], w_in[:, :CAST_SPLIT])
        nc.scalar.copy(w_out[:, CAST_SPLIT:], w_in[:, CAST_SPLIT:])
        xq_scales = gather_scales(offs_sb, S, "xq_scales")
        w_codes = new([P, H], U32, "w_codes")
        w_scales = new([P, H], U8, "w_scales")
        nc.vector.quantize_mx(out=w_codes[:].bitcast(FP8X4), scales=w_scales[:], in_=w_bf[:])

        xq_words = gather_words(offs_sb, S, "xq_words")
        hc_words = deal(gather_words(hc_sb, C, "hc_words_got"), U32, "hc_words")

        y = []
        for t in range(PACK):
            y_acc = product(t, w_codes, w_scales, t, xq_words[:], xq_scales[:])
            y.append(new([P, S], F32, "y%d" % t))
            if t == 0:
                nc.scalar.copy(y[t][:], y_acc[:])
            else:
                nc.vector.tensor_copy(y[t][:], y_acc[:])

        rb, a_win = [], []
        radicand = new([P, PACK * W], F32, "radicand")
        for t in range(PACK):
            a_win.append(new([P, 2 * S], F32, "a_win%d" % t))
            pair = a_win[t][:, S:]
            pa, pb = pair[:, :W], pair[:, W:]
            nc.scalar.activation(pa, y[t][:].indirect(n1_sb[:]), ACT.Copy)
            nc.scalar.activation(pb, y[t][:].indirect(n2_sb[:]), ACT.Copy)
            squares = new([P, 2 * W], F32, "squares%d" % t)
            rb.append(new([P, W], F32, "rb%d" % t))
            if t < LAST:
                nc.vector.scalar_tensor_tensor(rb[t][:], pa, -0.5, pb, ALU.mult, ALU.add)
            nc.vector.tensor_tensor(squares[:], pair, pair, ALU.mult)
            nc.vector.scalar_tensor_tensor(radicand[:, t * W:(t + 1) * W], squares[:, :W], 0.25, squares[:, W:], ALU.add, ALU.add)
            if t == LAST:
                nc.vector.scalar_tensor_tensor(rb[t][:], pa, -0.5, pb, ALU.mult, ALU.add)

        hc_scales = deal(gather_scales(hc_sb, C, "hc_scales_got", "y2"), U8, "hc_scales")
        for r in range(2):
            nc.sync.dma_start(hc_scales[2 + r:P:QUADRANT, :].bitcast(I32), hc_scales[GROUP + r:P:QUADRANT, :].bitcast(I32))
        ca_words = deal(gather_words(ca_sb, C, "ca_words_got", "squares3"), U32, "ca_words")
        ca_scales = deal(gather_scales(ca_sb, C, "ca_scales_got", "y3"), U8, "ca_scales")

        ra = new([P, PACK * W], F32, "ra")
        nc.scalar.activation(ra[:], radicand[:], ACT.Sqrt)
        dt = [new([P, S], F32, "dt%d" % t) for t in range(PACK)]
        for t in range(PACK):
            nc.scalar.activation(dt[t][:].indirect(n2_sb[:]), rb[t][:], ACT.Copy)
        z_bf = new([P, S * PACK], BF16, "z_bf")
        z_slots = z_bf[:].rearrange("p (c t) -> p t c", t=PACK)
        for t in range(PACK):
            nc.scalar.activation(dt[t][:].indirect(n1_sb[:]), ra[:, t * W:(t + 1) * W], ACT.Copy)
            for cols in spans(2 if t == LAST else 1):
                nc.vector.tensor_scalar(z_slots[:, t, cols], dt[t][:, cols], gs_sb[:, t:t + 1], None, ALU.mult)

        tanh_warm_out = new([P, 1], F32, "tanh_warm_out")
        nc.scalar.activation(tanh_warm_out[:], dt[LAST - 1][:, :1], ACT.Tanh)

        z_codes = new([P, S], U32, "z_codes")
        z_scales = new([P, S], U8, "z_scales")
        for cols in spans(2):
            nc.vector.quantize_mx(out=z_codes[:, cols].bitcast(FP8X4), scales=z_scales[:, cols],
                                  in_=z_bf[:, cols.start * PACK:cols.stop * PACK])

        b_win = []
        for t in range(PACK):
            b_win.append(new([P, 2 * S], F32, "b_win%d" % t))
            for cols in spans(2 if t == 0 else 1):
                bank = PACK + t if cols.stop == S else 0
                b_acc = product(bank, hc_words, hc_scales, t, z_codes[:, cols], z_scales[:, cols])
                nc.scalar.activation(b_win[t][:, S:][:, cols], b_acc[:], ACT.Tanh, scale=SCORE_SCALE)
                nc.vector.tensor_scalar(b_win[t][:, cols], b_acc[:], SCORE_SCALE, None, ALU.mult)
        for t in range(PACK):
            a_acc = product(PACK + t, ca_words, ca_scales, t, z_codes[:], z_scales[:])
            nc.vector.tensor_scalar(a_win[t][:, :S], a_acc[:], SCORE_SCALE, None, ALU.mult)

        out_rows = out.rearrange("(p t) c -> p t c", t=PACK)
        damped = []

        def fetch_b(t):
            gb = new([P, S], F32, "gb%d" % t)
            nc.scalar.activation(gb[:], b_win[t][:].indirect(n4_sb[:]), ACT.Copy)
            damped.append(new([P, S], F32, "damped%d" % t))
            nc.vector.tensor_tensor(damped[t][:], b_win[t][:, S:], gb[:], ALU.mult)

        def fetch_a_and_store(t, cols):
            width = cols.stop - cols.start
            ga = new([P, width], F32, "ga%d_%d" % (t, cols.start))
            offsets = n3_sb[:, cols.start // GROUP:cols.stop // GROUP]
            nc.scalar.activation(ga[:], a_win[t][:].indirect(offsets), ACT.Copy)
            result = new([P, width], F32, "result%d_%d" % (t, cols.start))
            nc.vector.tensor_tensor(result[:], ga[:], damped[t][:, cols], ALU.subtract)
            nc.sync.dma_start(out_rows[:, t, cols], result[:])

        fetch_b(0)
        for t in range(PACK):
            if t < LAST:
                fetch_b(t + 1)
            for cols in spans(2 if t == LAST else 1):
                fetch_a_and_store(t, cols)
